import numpy as np
CORES = [1,9,17,25,33,41,49,57,65,73,81,89,97,105,113,121]
N = 16
ROOT = 9
def setup_inputs(rng):
    return {"x": rng.standard_normal((N, 128, 8), dtype=np.float32)}
def reference(x):
    y = np.full((N, 128, N * 8), np.nan, x.dtype)
    y[ROOT] = np.concatenate(list(x), axis=1)
    return {"y": y}

@@ -1,0 +1,54 @@
+W = 8
+ROOT_RANK = 9
+
+SCRATCH = {
+    "stage": ("dram", [128, W], "float32"),
+    "relay": ("dram", [128, W], "float32"),
+    "land": ("sbuf", [128, 16 * W], "float32"),
+}
+SEMAPHORES = ["loaded", "read", "arrived", "stored"]
+
+FAR_DIE_CHIPS = (0, 4, 10, 14)
+
+
+def relay_core(chip):
+    return chip * 8 + (6 if chip in FAR_DIE_CHIPS else 2)
+
+
+def engines(mask):
+    return bin(mask).count("1")
+
+
+def send(g, T, topo, src, dst, out_ap, in_ap):
+    rid, pid, se = topo.addr(dst)
+    m = topo.mask(src, dst)
+    g.remote_dma(out_ap, in_ap, T.sem.arrived, T.sem.read, pid, rid, m)
+    g.wait_ge(T.sem.read, engines(m))
+
+
+def rank_program(g, core, T, topo):
+    root = T.cores[ROOT_RANK]
+    rank = T.rank_of(core)
+    chip = topo.chip(core)
+
+    if rank is None:
+        if chip % 2 == 0 and core == relay_core(chip):
+            j = T.rank_of(chip * 8 + 1)
+            g.wait_ge(T.sem.arrived, engines(topo.mask(chip * 8 + 1, core)))
+            send(g, T, topo, core, root, T.land[:, W * j:W * (j + 1)], T.relay[:])
+        return
+
+    if core == root:
+        g.dma_start(T.land[:, W * rank:W * (rank + 1)], T.x[:]).then_inc(T.sem.loaded, 16)
+        g.wait_ge(T.sem.arrived, 15 * engines(0x00FF))
+        g.wait_ge(T.sem.loaded, 16)
+        g.dma_start(T.y[:], T.land[:]).then_inc(T.sem.stored, 16)
+        g.wait_ge(T.sem.stored, 16)
+        return
+
+    g.dma_start(T.stage[:], T.x[:]).then_inc(T.sem.loaded, 16)
+    g.wait_ge(T.sem.loaded, 16)
+    if topo.may_write(core, root):
+        send(g, T, topo, core, root, T.land[:, W * rank:W * (rank + 1)], T.stage[:])
+    else:
+        send(g, T, topo, core, relay_core(chip), T.relay[:], T.stage[:])

@@ -8,11 +8,9 @@ SCRATCH = {
 }
 SEMAPHORES = ["loaded", "read", "arrived", "stored"]
 
-FAR_DIE_CHIPS = (0, 4, 10, 14)
-
 
 def relay_core(chip):
-    return chip * 8 + (6 if chip in FAR_DIE_CHIPS else 2)
+    return chip * 8 + 2
 
 
 def engines(mask):

W = 8
ROOT_RANK = 9

SCRATCH = {
    "stage": ("dram", [128, W], "float32"),
    "relay": ("dram", [128, W], "float32"),
    "land": ("sbuf", [128, 16 * W], "float32"),
}
SEMAPHORES = ["loaded", "read", "arrived", "stored"]


def relay_core(chip):
    return chip * 8 + 2


def engines(mask):
    return bin(mask).count("1")


def send(g, T, topo, src, dst, out_ap, in_ap):
    rid, pid, se = topo.addr(dst)
    m = topo.mask(src, dst)
    g.remote_dma(out_ap, in_ap, T.sem.arrived, T.sem.read, pid, rid, m)
    g.wait_ge(T.sem.read, engines(m))


def rank_program(g, core, T, topo):
    root = T.cores[ROOT_RANK]
    rank = T.rank_of(core)
    chip = topo.chip(core)

    if rank is None:
        if chip % 2 == 0 and core == relay_core(chip):
            j = T.rank_of(chip * 8 + 1)
            g.wait_ge(T.sem.arrived, engines(topo.mask(chip * 8 + 1, core)))
            send(g, T, topo, core, root, T.land[:, W * j:W * (j + 1)], T.relay[:])
        return

    if core == root:
        g.dma_start(T.land[:, W * rank:W * (rank + 1)], T.x[:]).then_inc(T.sem.loaded, 16)
        g.wait_ge(T.sem.arrived, 15 * engines(0x00FF))
        g.wait_ge(T.sem.loaded, 16)
        g.dma_start(T.y[:], T.land[:]).then_inc(T.sem.stored, 16)
        g.wait_ge(T.sem.stored, 16)
        return

    g.dma_start(T.stage[:], T.x[:]).then_inc(T.sem.loaded, 16)
    g.wait_ge(T.sem.loaded, 16)
    if topo.may_write(core, root):
        send(g, T, topo, core, root, T.land[:, W * rank:W * (rank + 1)], T.stage[:])
    else:
        send(g, T, topo, core, relay_core(chip), T.relay[:], T.stage[:])
